import numpy as np
import ml_dtypes


def mxq(x, axis, fmt="e4m3"):
    dtype, down = {"e4m3": (ml_dtypes.float8_e4m3fn, 7), "e5m2": (ml_dtypes.float8_e5m2, 14)}[fmt]
    v = np.moveaxis(np.asarray(x, np.float32).astype(ml_dtypes.bfloat16).astype(np.float64), axis, -1)
    blocks = v.reshape(v.shape[:-1] + (-1, 32))
    amax = np.abs(blocks).max(-1, keepdims=True)
    byte = np.maximum(np.where(amax > 0, np.frexp(amax)[1] - 1 + 127, 0) - down, 1)
    scale = np.exp2(byte - 127.0)
    codes = (blocks / scale).astype(np.float32).astype(dtype).astype(np.float64)
    return np.moveaxis((codes * scale).reshape(v.shape), -1, axis)


WIDE = False


def mx_kscale(k):
    if not WIDE:
        return np.ones(k)
    levels = np.array([10, -10, 5, -5, 0])
    if k % 512:
        return np.exp2(np.random.permutation(np.resize(levels, k // 32))).repeat(32)
    a = np.empty((k // 512, 16))
    for p in range(k // 512):
        a[p, :8] = np.random.permutation(np.resize(levels, 8))
        for g in range(8):
            far = levels[np.abs(levels - a[p, g]) >= 10]
            a[p, g + 8] = far[np.random.randint(len(far))]
    return np.exp2(a.ravel()).repeat(32)


BF16 = ml_dtypes.bfloat16


def bf(x):
    return np.asarray(x, np.float32).astype(BF16)


def f64(x):
    return np.asarray(x).astype(np.float64)


E2M1 = np.array([0.0, 0.5, 1.0, 1.5, 2.0, 3.0, 4.0, 6.0, -0.0, -0.5, -1.0, -1.5, -2.0, -3.0, -4.0, -6.0])


def pack_weight(w, fmt):
    k, n = w.shape
    w = f64(bf(w)).reshape(k // 32, 32, n)
    amax = np.abs(w).max(1)
    if fmt == "e4m3":
        byte = np.frexp(amax)[1] - 1 + 127 - 7
    else:
        mant, ex = np.frexp(amax / 6.0)
        byte = np.where(mant > 0.5, ex, ex - 1) + 127
    byte = np.clip(np.where(amax > 0, byte, 1), 1, 254)
    scaled = (w * np.exp2(127.0 - byte)[:, None, :]).reshape(k, n).astype(np.float32)
    by_word = np.ascontiguousarray(scaled.reshape(k // 512, 128, 4, n).transpose(0, 1, 3, 2))
    if fmt == "e4m3":
        words = by_word.astype(ml_dtypes.float8_e4m3fn).view(np.uint8)
    else:
        c = by_word.astype(ml_dtypes.float4_e2m1fn).view(np.uint8) & 0xF
        words = c[..., 0::2] | (c[..., 1::2] << 4)
    return np.ascontiguousarray(words), np.ascontiguousarray(byte.astype(np.uint8).reshape(k // 512, 16, n))


def unpack_weight(words, scales, fmt):
    g, p, n, _ = words.shape
    if fmt == "e4m3":
        vals = np.ascontiguousarray(words).view(ml_dtypes.float8_e4m3fn).astype(np.float64)
    else:
        nib = np.empty((g, p, n, 4), np.uint8)
        nib[..., 0::2] = words & 0xF
        nib[..., 1::2] = words >> 4
        vals = E2M1[nib]
    vals = vals * np.repeat(np.exp2(scales.astype(np.float64) - 127.0), 8, axis=1)[..., None]
    return vals.transpose(0, 1, 3, 2).reshape(g * 512, n)
def pack4(w):
    words, scales = pack_weight(w, "e2m1")
    return words.reshape(words.shape[0], 128, -1), scales


def unpack4(words, scales):
    return unpack_weight(words.reshape(words.shape[0], 128, -1, 2), scales, "e2m1")


E4M3FN = np.array([(-1.0 if i & 128 else 1.0) * ((1.0 + (i & 7) / 8.0) * 2.0 ** (((i >> 3) & 15) - 7) if i & 120 else (i & 7) * 2.0 ** -9) for i in range(256)])


def e4m3fn_bytes(y):
    return np.clip(np.asarray(y, np.float64), -448.0, 448.0).astype(np.float32).astype(ml_dtypes.float8_e4m3fn).view(np.uint8)


def e4m3fn_values(b):
    return E4M3FN[b]


T, N, J, K, P = 1024, 1024, 1024, 128, 512


def soft_threshold(e, t):
    return np.sign(e) * np.maximum(np.abs(e) - t, 0.0)


def draw0():
    s = mx_kscale(T)
    u = mx_kscale(N)
    a = 0.88 * T**0.25
    inputs = {"x": bf(np.random.standard_normal((T, N)) * a * s[:, None]),
              "y": bf(np.random.standard_normal((T, J)) * a / s[:, None]),
              "l": bf(np.random.standard_normal((N, K))),
              "m": bf(np.random.standard_normal((K, J)) / np.sqrt(K)),
              "tau": bf(np.random.uniform(0.3, 0.9, N)),
              "g": bf((1.0 + 0.1 * np.random.standard_normal(N)) * u)}
    w = np.random.standard_normal((P, N)) / np.sqrt(N) / u[None, :]
    words, scales = pack4(w.T)
    inputs["w_words"] = words
    inputs["w_scales"] = scales
    return inputs


def core(x, y, l, m, tau, g, w_words, w_scales):
    xq = mxq(f64(x), 0, "e4m3")
    yq = mxq(f64(y), 0, "e4m3")
    c = (xq.T @ yq) / x.shape[0]
    f = f64(l) @ f64(m)
    e = c - f
    th = soft_threshold(e, f64(tau)[:, None])
    sig = f64(g)[:, None] * (f + th)
    return unpack4(w_words, w_scales).T @ mxq(sig, 0, "e4m3")


def setup_inputs():
    drawn = draw0()
    full = np.asarray(drawn['y']).astype(np.float64)
    scale = (np.abs(full).reshape(8, 128, 8, 128).max(axis=(1, 3)) / 448.0).astype(np.float32)
    given = {}
    for key, value in drawn.items():
        if key == 'y':
            given['y_bytes'] = e4m3fn_bytes(full / np.repeat(np.repeat(scale.astype(np.float64), 128, axis=0), 128, axis=1))
            given['y_scale'] = scale
        else:
            given[key] = value
    return given


def reference(x, y_bytes, y_scale, l, m, tau, g, w_words, w_scales):
    return core(x, e4m3fn_values(y_bytes) * np.repeat(np.repeat(y_scale.astype(np.float64), 128, axis=0), 128, axis=1), l, m, tau, g, w_words, w_scales)

@@ -1,0 +1,307 @@
+from contextlib import ExitStack
+
+import concourse.mybir as mybir
+from concourse.masks import make_identity
+
+F32 = mybir.dt.float32
+BF16 = mybir.dt.bfloat16
+U8 = mybir.dt.uint8
+U32 = mybir.dt.uint32
+I32 = mybir.dt.int32
+FP8 = mybir.dt.float8_e4m3fn
+FP8X4 = mybir.dt.float8_e4m3fn_x4
+FP4X4 = mybir.dt.float4_e2m1fn_x4
+ALU = mybir.AluOpType
+COPY = mybir.ActivationFunctionType.Copy
+
+T, N, J, K, P = 1024, 1024, 1024, 128, 512
+FLOPS = 2 * T * N * J + 2 * N * K * J + 2 * P * N * J
+H = 512
+
+
+def tile_lowrankplussoftthresholdedcrosscovarianc_d2p_kernel(
+    tc, x, y_bytes, y_scale, l, m, tau, g, w_words, w_scales, out
+):
+    nc = tc.nc
+    with ExitStack() as ctx:
+        keep = ctx.enter_context(tc.tile_pool(name="keep", bufs=1))
+        work = ctx.enter_context(tc.tile_pool(name="work", bufs=2))
+        deep = ctx.enter_context(tc.tile_pool(name="deep", bufs=8))
+        psum = ctx.enter_context(tc.psum_pool(name="psum", bufs=8))
+        ctx.enter_context(tc.manual_schedule())
+
+        x_v = x.rearrange("(q p j) n -> q p j n", q=2, p=128, j=4)
+        y_v = y_bytes.rearrange("(q p j) n -> q p j n", q=2, p=128, j=4)
+
+        x_raw = {(q, s): keep.tile([128, 4, H], BF16, name=f"x_raw_{q}{s}", align_bytes=64) for q in range(2) for s in range(2)}
+        y_raw = {(q, h): keep.tile([128, 4, H], U8, name=f"y_raw_{q}{h}", align_bytes=64) for q in range(2) for h in range(2)}
+        x_code = {(q, s): keep.tile([128, H], U32, name=f"x_code_{q}{s}", align_bytes=64) for q in range(2) for s in range(2)}
+        x_sc = {(q, s): keep.tile([128, H], U8, name=f"x_sc_{q}{s}", align_bytes=64) for q in range(2) for s in range(2)}
+        y_code = {(q, h): keep.tile([128, H], U32, name=f"y_code_{q}{h}", align_bytes=64) for q in range(2) for h in range(2)}
+        y_sc = {(q, h): keep.tile([128, H], U8, name=f"y_sc_{q}{h}", align_bytes=64) for q in range(2) for h in range(2)}
+        s_code = {(s, h): keep.tile([128, H], U32, name=f"s_code_{s}{h}", align_bytes=64) for s in range(2) for h in range(2)}
+        s_sc = {(s, h): keep.tile([128, H], U8, name=f"s_sc_{s}{h}", align_bytes=64) for s in range(2) for h in range(2)}
+        f_sb = {(s, t, h): keep.tile([128, H], F32, name=f"f_sb_{s}{t}{h}") for s in range(2) for t in range(4) for h in range(2)}
+        l_sb = keep.tile([128, 2, 4, K], BF16, name="l_sb")
+        m_sb = keep.tile([K, J], BF16, name="m_sb")
+        lT = keep.tile([K, 8, 128], BF16, name="lT")
+        ident = keep.tile([128, 128], BF16, name="ident")
+        ysc = keep.tile([128, 2, 8], F32, name="ysc")
+        g_b = keep.tile([128, 8], BF16, name="g_b")
+        t_b = keep.tile([128, 8], BF16, name="t_b")
+        gf = keep.tile([128, 8], F32, name="gf")
+        gs = keep.tile([128, 8], F32, name="gs")
+        gt = keep.tile([128, 8], F32, name="gt")
+        ngt = keep.tile([128, 8], F32, name="ngt")
+        hi = keep.tile([128, 8], F32, name="hi")
+        lo = keep.tile([128, 8], F32, name="lo")
+        ww = keep.tile([128, 2, 2 * P], U8, name="ww", align_bytes=64)
+        wsc = keep.tile([128, 2, P], U8, name="wsc", align_bytes=64)
+
+        def load_x(q, s):
+            nc.sync.dma_start(out=x_raw[q, s][:], in_=x_v[q][:, :, s * H : (s + 1) * H])
+
+        def load_y(q, h):
+            nc.sync.dma_start(out=y_raw[q, h][:], in_=y_v[q][:, :, h * H : (h + 1) * H])
+
+        load_x(0, 0)
+        load_y(0, 0)
+        load_x(1, 0)
+        load_y(1, 0)
+        nc.sync.dma_start(out=l_sb[:], in_=l.rearrange("(s p t) k -> p s t k", s=2, p=128, t=4))
+        nc.sync.dma_start(out=m_sb[:], in_=m)
+        load_x(0, 1)
+        load_x(1, 1)
+        load_y(0, 1)
+        load_y(1, 1)
+        nc.sync.dma_start(out=ww[:].bitcast(I32), in_=w_words.bitcast(I32).rearrange("s p n -> p s n"))
+
+        nc.scalar.dma_start(out=g_b[:].rearrange("p (s t) -> p s t", s=2), in_=g.rearrange("(s p t) -> p s t", s=2, p=128, t=4))
+        nc.scalar.dma_start(out=t_b[:].rearrange("p (s t) -> p s t", s=2), in_=tau.rearrange("(s p t) -> p s t", s=2, p=128, t=4))
+        for i in range(4):
+            nc.scalar.dma_start(
+                out=ysc[32 * i : 32 * i + 32], in_=y_scale.rearrange("(q i) b -> i q b", i=4)[i].partition_broadcast(32)
+            )
+
+        make_identity(nc, ident[:])
+        nc.gpsimd.memset(wsc[:].bitcast(I32), 0)
+        for i in range(4):
+            nc.gpsimd.dma_start(
+                out=wsc[32 * i : 32 * i + 4].bitcast(I32),
+                in_=w_scales[:, 4 * i : 4 * i + 4, :].bitcast(I32).rearrange("s r n -> r s n"),
+            )
+
+        xi = {}
+        yw = {}
+        yi = {}
+        bank = {}
+        e_sb = {}
+        k_sb = {}
+        sg = {}
+        si = {}
+
+        def x_lay(q, s):
+            xi[q, s] = work.tile([128, 4 * H], BF16, name="xi", bufs=4, align_bytes=64)
+            nc.vector.tensor_copy(
+                out=xi[q, s][:].rearrange("p (t m j) -> p t m j", t=4, j=4),
+                in_=x_raw[q, s][:].rearrange("p j (m t) -> p t m j", t=4),
+            )
+
+        def x_quant(q, s):
+            nc.vector.quantize_mx(out=x_code[q, s][:].bitcast(FP8X4), scales=x_sc[q, s][:], in_=xi[q, s][:])
+
+        def y_widen(q, h):
+            yw[q, h] = work.tile([128, 4, H], BF16, name="yw", bufs=4, align_bytes=64)
+            nc.scalar.copy(
+                out=yw[q, h][:].rearrange("p j n -> p (j n)"), in_=y_raw[q, h][:].rearrange("p j n -> p (j n)").bitcast(FP8)
+            )
+
+        def y_lay_scalar(q, h):
+            yi[q, h] = work.tile([128, H, 4], BF16, name="yi", bufs=4, align_bytes=64)
+            for b in range(4):
+                cols = slice(128 * b, 128 * b + 128)
+                nc.scalar.activation(
+                    out=yi[q, h][:, cols, :].rearrange("p (c i) j -> p c j i", i=4),
+                    in_=yw[q, h][:, :, cols].rearrange("p j (c i) -> p c j i", i=4),
+                    func=COPY,
+                    scale=ysc[:, q, 4 * h + b : 4 * h + b + 1],
+                )
+
+        def y_lay(q, h):
+            yi[q, h] = work.tile([128, H, 4], BF16, name="yi", bufs=4, align_bytes=64)
+            for b in range(4):
+                cols = slice(128 * b, 128 * b + 128)
+                nc.vector.tensor_scalar(
+                    out=yi[q, h][:, cols, :].rearrange("p (c i) j -> p c j i", i=4),
+                    in0=yw[q, h][:, :, cols].rearrange("p j (c i) -> p c j i", i=4),
+                    scalar1=ysc[:, q, 4 * h + b : 4 * h + b + 1],
+                    scalar2=None,
+                    op0=ALU.mult,
+                )
+
+        def y_quant(q, h):
+            nc.vector.quantize_mx(
+                out=y_code[q, h][:].bitcast(FP8X4), scales=y_sc[q, h][:], in_=yi[q, h][:].rearrange("p n j -> p (n j)")
+            )
+
+        def low_rank_weights():
+            for s in range(2):
+                ps = psum.tile([128, 512], BF16, name="ps_l", tag="ps")
+                for t in range(4):
+                    nc.tensor.transpose(ps[:, 128 * t : 128 * t + 128], l_sb[:, s, t, :], ident[:])
+                nc.scalar.copy(out=lT[:, 4 * s : 4 * s + 4, :].rearrange("p t n -> p (t n)"), in_=ps[:])
+
+        def low_rank(s, h):
+            for t in range(4):
+                ps = psum.tile([128, H], F32, name="ps_f", tag="ps")
+                nc.tensor.matmul(ps[:], lT[:, 4 * s + t, :], m_sb[:, h * H : (h + 1) * H], start=True, stop=True)
+                nc.scalar.activation(out=f_sb[s, t, h][:], in_=ps[:], func=COPY, scale=gf[:, 4 * s + t : 4 * s + t + 1])
+
+        def cross(s, h):
+            for t in range(4):
+                ps = psum.tile([128, H], F32, name="ps_c", tag="ps")
+                bank[s, t, h] = ps
+                for q in range(2):
+                    nc.tensor.matmul_mx(
+                        out=ps[:],
+                        lhsT=x_code[q, s][:, 128 * t : 128 * t + 128].bitcast(FP8X4),
+                        lhsT_scale=x_sc[q, s][:, 128 * t : 128 * t + 128],
+                        rhs=y_code[q, h][:].bitcast(FP8X4),
+                        rhs_scale=y_sc[q, h][:],
+                        start=(q == 0),
+                        stop=(q == 1),
+                    )
+
+        def diff(s, h):
+            for t in range(4):
+                col = slice(4 * s + t, 4 * s + t + 1)
+                e = deep.tile([128, H], F32, name="e_sb")
+                k = deep.tile([128, H], F32, name="k_sb")
+                k_sb[s, t, h] = k
+                nc.vector.scalar_tensor_tensor(
+                    out=e[:], in0=bank[s, t, h][:], scalar=gs[:, col], in1=f_sb[s, t, h][:], op0=ALU.mult, op1=ALU.subtract
+                )
+                nc.gpsimd.tensor_scalar(
+                    out=k[:], in0=e[:], scalar1=hi[:, col], scalar2=lo[:, col], op0=ALU.min, op1=ALU.max
+                )
+
+        def shrink(s, h, parts):
+            sg[s, h] = work.tile([128, 4, H], BF16, name="sg", bufs=3, align_bytes=64)
+            w = H // parts
+            for c in range(parts):
+                cols = slice(c * w, c * w + w)
+                for t in range(4):
+                    nc.vector.scalar_tensor_tensor(
+                        out=sg[s, h][:, t, cols],
+                        in0=bank[s, t, h][:, cols],
+                        scalar=gs[:, 4 * s + t : 4 * s + t + 1],
+                        in1=k_sb[s, t, h][:, cols],
+                        op0=ALU.mult,
+                        op1=ALU.subtract,
+                    )
+
+        def s_lay(s, h, lo_c, hi_c, engine_copy):
+            if (s, h) not in si:
+                si[s, h] = work.tile([128, H, 4], BF16, name="si", bufs=3, align_bytes=64)
+            engine_copy(
+                out=si[s, h][:, lo_c:hi_c, :].rearrange("p (c i) t -> p c t i", i=4),
+                in_=sg[s, h][:, :, lo_c:hi_c].rearrange("p t (c i) -> p c t i", i=4),
+            )
+
+        def s_quant(s, h, lo_c, hi_c):
+            nc.vector.quantize_mx(
+                out=s_code[s, h][:, lo_c:hi_c].bitcast(FP8X4),
+                scales=s_sc[s, h][:, lo_c:hi_c],
+                in_=si[s, h][:, lo_c:hi_c, :].rearrange("p n t -> p (n t)"),
+            )
+
+        acc = {}
+
+        def exposure(s, h):
+            for b in range(4):
+                if s == 0:
+                    acc[b, h] = psum.tile([128, H], F32, name="ps_o", tag="ps")
+                nc.tensor.matmul_mx(
+                    out=acc[b, h][:],
+                    lhsT=ww[:, s, 256 * b : 256 * b + 256].bitcast(FP4X4),
+                    lhsT_scale=wsc[:, s, 128 * b : 128 * b + 128],
+                    rhs=s_code[s, h][:].bitcast(FP8X4),
+                    rhs_scale=s_sc[s, h][:],
+                    start=(s == 0),
+                    stop=(s == 1),
+                )
+
+        def store(h, vector_too):
+            for b in range(4):
+                o = deep.tile([128, H], F32, name="o_sb")
+                if vector_too and b % 2 == 1:
+                    nc.vector.tensor_copy(out=o[:], in_=acc[b, h][:])
+                else:
+                    nc.scalar.copy(out=o[:], in_=acc[b, h][:])
+                nc.sync.dma_start(out=out[128 * b : 128 * b + 128, h * H : (h + 1) * H], in_=o[:])
+
+        def row_factors():
+            nc.vector.tensor_copy(out=gf[:], in_=g_b[:])
+            nc.vector.tensor_tensor(out=gt[:], in0=g_b[:], in1=t_b[:], op=ALU.mult)
+            nc.vector.tensor_scalar(out=gs[:], in0=gf[:], scalar1=1.0 / T, scalar2=None, op0=ALU.mult)
+            nc.vector.tensor_scalar(out=ngt[:], in0=gt[:], scalar1=-1.0, scalar2=None, op0=ALU.mult)
+            nc.vector.tensor_tensor(out=hi[:], in0=gt[:], in1=ngt[:], op=ALU.max)
+            nc.vector.tensor_tensor(out=lo[:], in0=gt[:], in1=ngt[:], op=ALU.min)
+
+        vcopy = nc.vector.tensor_copy
+        scopy = nc.scalar.copy
+
+        x_lay(0, 0)
+        row_factors()
+        y_widen(0, 0)
+        x_lay(1, 0)
+        y_widen(1, 0)
+        x_quant(0, 0)
+        x_quant(1, 0)
+        low_rank_weights()
+        y_lay(0, 0)
+        y_lay(1, 0)
+        low_rank(0, 0)
+        y_quant(0, 0)
+        y_quant(1, 0)
+        cross(0, 0)
+        low_rank(1, 0)
+        x_lay(0, 1)
+        x_lay(1, 1)
+        x_quant(0, 1)
+        diff(0, 0)
+        x_quant(1, 1)
+        y_widen(0, 1)
+        y_widen(1, 1)
+        shrink(0, 0, 1)
+        cross(1, 0)
+        y_lay_scalar(1, 1)
+        low_rank(0, 1)
+        y_lay(0, 1)
+        diff(1, 0)
+        y_quant(0, 1)
+        y_quant(1, 1)
+        s_lay(0, 0, 0, H, scopy)
+        cross(0, 1)
+        low_rank(1, 1)
+        shrink(1, 0, 1)
+        s_lay(1, 0, 0, H, scopy)
+        diff(0, 1)
+        s_quant(0, 0, 0, H)
+        exposure(0, 0)
+        shrink(0, 1, 1)
+        s_quant(1, 0, 0, H)
+        cross(1, 1)
+        exposure(1, 0)
+        s_lay(0, 1, 0, H, scopy)
+        diff(1, 1)
+        store(0, False)
+        s_quant(0, 1, 0, H)
+        shrink(1, 1, 2)
+        exposure(0, 1)
+        s_lay(1, 1, 0, 256, scopy)
+        s_lay(1, 1, 256, H, vcopy)
+        s_quant(1, 1, 0, 256)
+        s_quant(1, 1, 256, H)
+        exposure(1, 1)
+        store(1, True)

@@ -58,13 +58,17 @@ def tile_lowrankplussoftthresholdedcrosscovarianc_d2p_kernel(
         ww = keep.tile([128, 2, 2 * P], U8, name="ww", align_bytes=64)
         wsc = keep.tile([128, 2, P], U8, name="wsc", align_bytes=64)
 
-        def load_x(q, s):
-            nc.sync.dma_start(out=x_raw[q, s][:], in_=x_v[q][:, :, s * H : (s + 1) * H])
+        def load_x(q, s, parts=1):
+            w = H // parts
+            for c in range(parts):
+                nc.sync.dma_start(
+                    out=x_raw[q, s][:, :, c * w : (c + 1) * w], in_=x_v[q][:, :, s * H + c * w : s * H + (c + 1) * w]
+                )
 
         def load_y(q, h):
             nc.sync.dma_start(out=y_raw[q, h][:], in_=y_v[q][:, :, h * H : (h + 1) * H])
 
-        load_x(0, 0)
+        load_x(0, 0, 2)
         load_y(0, 0)
         load_x(1, 0)
         load_y(1, 0)
@@ -100,12 +104,13 @@ def tile_lowrankplussoftthresholdedcrosscovarianc_d2p_kernel(
         sg = {}
         si = {}
 
-        def x_lay(q, s):
+        def x_lay(q, s, engine_copy=nc.vector.tensor_copy, parts=1):
             xi[q, s] = work.tile([128, 4 * H], BF16, name="xi", bufs=4, align_bytes=64)
-            nc.vector.tensor_copy(
-                out=xi[q, s][:].rearrange("p (t m j) -> p t m j", t=4, j=4),
-                in_=x_raw[q, s][:].rearrange("p j (m t) -> p t m j", t=4),
-            )
+            dst = xi[q, s][:].rearrange("p (t m j) -> p t m j", t=4, j=4)
+            src = x_raw[q, s][:].rearrange("p j (m t) -> p t m j", t=4)
+            w = 128 // parts
+            for c in range(parts):
+                engine_copy(out=dst[:, :, c * w : (c + 1) * w, :], in_=src[:, :, c * w : (c + 1) * w, :])
 
         def x_quant(q, s):
             nc.vector.quantize_mx(out=x_code[q, s][:].bitcast(FP8X4), scales=x_sc[q, s][:], in_=xi[q, s][:])
@@ -185,11 +190,11 @@ def tile_lowrankplussoftthresholdedcrosscovarianc_d2p_kernel(
                     out=k[:], in0=e[:], scalar1=hi[:, col], scalar2=lo[:, col], op0=ALU.min, op1=ALU.max
                 )
 
-        def shrink(s, h, parts):
-            sg[s, h] = work.tile([128, 4, H], BF16, name="sg", bufs=3, align_bytes=64)
-            w = H // parts
-            for c in range(parts):
-                cols = slice(c * w, c * w + w)
+        def shrink(s, h, lo_c, hi_c):
+            if (s, h) not in sg:
+                sg[s, h] = work.tile([128, 4, H], BF16, name="sg", bufs=3, align_bytes=64)
+            if True:
+                cols = slice(lo_c, hi_c)
                 for t in range(4):
                     nc.vector.scalar_tensor_tensor(
                         out=sg[s, h][:, t, cols],
@@ -240,6 +245,46 @@ def tile_lowrankplussoftthresholdedcrosscovarianc_d2p_kernel(
                     nc.scalar.copy(out=o[:], in_=acc[b, h][:])
                 nc.sync.dma_start(out=out[128 * b : 128 * b + 128, h * H : (h + 1) * H], in_=o[:])
 
+        def exposure_cols(bank_of, h, lo_c, hi_c):
+            for c in range(lo_c, hi_c, 128):
+                for b in range(4):
+                    for s in range(2):
+                        nc.tensor.matmul_mx(
+                            out=bank_of(b, c),
+                            lhsT=ww[:, s, 256 * b : 256 * b + 256].bitcast(FP4X4),
+                            lhsT_scale=wsc[:, s, 128 * b : 128 * b + 128],
+                            rhs=s_code[s, h][:, c : c + 128].bitcast(FP8X4),
+                            rhs_scale=s_sc[s, h][:, c : c + 128],
+                            start=(s == 0),
+                            stop=(s == 1),
+                        )
+
+        tail = {}
+
+        def exposure_main(h, lo_c, hi_c):
+            if lo_c == 0:
+                for b in range(4):
+                    tail[b] = psum.tile([128, H], F32, name="ps_m", tag="ps")
+            exposure_cols(lambda b, c: tail[b][:, c : c + 128], h, lo_c, hi_c)
+
+        def exposure_last(h):
+            for b in range(2):
+                tail[4 + b] = psum.tile([128, H], F32, name="ps_t", tag="ps")
+            exposure_cols(lambda b, c: tail[4 + b // 2][:, 128 * (b % 2) : 128 * (b % 2) + 128], h, H - 128, H)
+
+        def store_main(h, b, engine_copy):
+            o = deep.tile([128, H - 128], F32, name="o_main", bufs=4)
+            engine_copy(out=o[:], in_=tail[b][:, : H - 128])
+            nc.sync.dma_start(out=out[128 * b : 128 * b + 128, h * H : h * H + H - 128], in_=o[:])
+
+        def store_last(h):
+            for b, engine_copy in ((0, vcopy), (1, scopy)):
+                o = deep.tile([128, 2, 128], F32, name="o_last", bufs=2)
+                engine_copy(out=o[:].rearrange("p b n -> p (b n)"), in_=tail[4 + b][:, :256])
+                nc.sync.dma_start(
+                    out=out[256 * b : 256 * b + 256, h * H + H - 128 : h * H + H].rearrange("(b p) n -> p b n", b=2), in_=o[:]
+                )
+
         def row_factors():
             nc.vector.tensor_copy(out=gf[:], in_=g_b[:])
             nc.vector.tensor_tensor(out=gt[:], in0=g_b[:], in1=t_b[:], op=ALU.mult)
@@ -251,7 +296,7 @@ def tile_lowrankplussoftthresholdedcrosscovarianc_d2p_kernel(
         vcopy = nc.vector.tensor_copy
         scopy = nc.scalar.copy
 
-        x_lay(0, 0)
+        x_lay(0, 0, vcopy, 2)
         row_factors()
         y_widen(0, 0)
         x_lay(1, 0)
@@ -262,46 +307,55 @@ def tile_lowrankplussoftthresholdedcrosscovarianc_d2p_kernel(
         y_lay(0, 0)
         y_lay(1, 0)
         low_rank(0, 0)
+        low_rank(1, 0)
         y_quant(0, 0)
         y_quant(1, 0)
         cross(0, 0)
-        low_rank(1, 0)
         x_lay(0, 1)
         x_lay(1, 1)
         x_quant(0, 1)
-        diff(0, 0)
         x_quant(1, 1)
         y_widen(0, 1)
         y_widen(1, 1)
-        shrink(0, 0, 1)
+        diff(0, 0)
+        shrink(0, 0, 0, H)
         cross(1, 0)
         y_lay_scalar(1, 1)
         low_rank(0, 1)
         y_lay(0, 1)
-        diff(1, 0)
         y_quant(0, 1)
         y_quant(1, 1)
         s_lay(0, 0, 0, H, scopy)
-        cross(0, 1)
         low_rank(1, 1)
-        shrink(1, 0, 1)
+        diff(1, 0)
+        shrink(1, 0, 0, H)
+        cross(0, 1)
         s_lay(1, 0, 0, H, scopy)
-        diff(0, 1)
         s_quant(0, 0, 0, H)
-        exposure(0, 0)
-        shrink(0, 1, 1)
-        s_quant(1, 0, 0, H)
+        diff(0, 1)
+        shrink(0, 1, 0, H)
         cross(1, 1)
-        exposure(1, 0)
+        exposure(0, 0)
         s_lay(0, 1, 0, H, scopy)
-        diff(1, 1)
+        s_quant(1, 0, 0, H)
+        exposure(1, 0)
         store(0, False)
+        diff(1, 1)
         s_quant(0, 1, 0, H)
-        shrink(1, 1, 2)
-        exposure(0, 1)
+        shrink(1, 1, 0, 256)
+        shrink(1, 1, 256, 384)
         s_lay(1, 1, 0, 256, scopy)
-        s_lay(1, 1, 256, H, vcopy)
+        s_lay(1, 1, 256, 384, scopy)
+        shrink(1, 1, 384, H)
         s_quant(1, 1, 0, 256)
-        s_quant(1, 1, 256, H)
-        exposure(1, 1)
-        store(1, True)
+        exposure_main(1, 0, 256)
+        s_lay(1, 1, 384, H, vcopy)
+        s_quant(1, 1, 256, 384)
+        exposure_main(1, 256, 384)
+        s_quant(1, 1, 384, H)
+        exposure_last(1)
+        store_main(1, 0, scopy)
+        store_main(1, 1, vcopy)
+        store_main(1, 2, scopy)
+        store_main(1, 3, vcopy)
+        store_last(1)

@@ -51,8 +51,7 @@ def tile_lowrankplussoftthresholdedcrosscovarianc_d2p_kernel(
         t_b = keep.tile([128, 8], BF16, name="t_b")
         gf = keep.tile([128, 8], F32, name="gf")
         gs = keep.tile([128, 8], F32, name="gs")
-        gt = keep.tile([128, 8], F32, name="gt")
-        ngt = keep.tile([128, 8], F32, name="ngt")
+        ga = keep.tile([128, 8], F32, name="ga")
         hi = keep.tile([128, 8], F32, name="hi")
         lo = keep.tile([128, 8], F32, name="lo")
         ww = keep.tile([128, 2, 2 * P], U8, name="ww", align_bytes=64)
@@ -70,7 +69,7 @@ def tile_lowrankplussoftthresholdedcrosscovarianc_d2p_kernel(
 
         load_x(0, 0, 2)
         load_y(0, 0)
-        load_x(1, 0)
+        load_x(1, 0, 2)
         load_y(1, 0)
         nc.sync.dma_start(out=l_sb[:], in_=l.rearrange("(s p t) k -> p s t k", s=2, p=128, t=4))
         nc.sync.dma_start(out=m_sb[:], in_=m)
@@ -121,9 +120,10 @@ def tile_lowrankplussoftthresholdedcrosscovarianc_d2p_kernel(
                 out=yw[q, h][:].rearrange("p j n -> p (j n)"), in_=y_raw[q, h][:].rearrange("p j n -> p (j n)").bitcast(FP8)
             )
 
-        def y_lay_scalar(q, h):
-            yi[q, h] = work.tile([128, H, 4], BF16, name="yi", bufs=4, align_bytes=64)
-            for b in range(4):
+        def y_lay_scalar(q, h, blocks=range(4)):
+            if (q, h) not in yi:
+                yi[q, h] = work.tile([128, H, 4], BF16, name="yi", bufs=4, align_bytes=64)
+            for b in blocks:
                 cols = slice(128 * b, 128 * b + 128)
                 nc.scalar.activation(
                     out=yi[q, h][:, cols, :].rearrange("p (c i) j -> p c j i", i=4),
@@ -132,9 +132,10 @@ def tile_lowrankplussoftthresholdedcrosscovarianc_d2p_kernel(
                     scale=ysc[:, q, 4 * h + b : 4 * h + b + 1],
                 )
 
-        def y_lay(q, h):
-            yi[q, h] = work.tile([128, H, 4], BF16, name="yi", bufs=4, align_bytes=64)
-            for b in range(4):
+        def y_lay(q, h, blocks=range(4)):
+            if (q, h) not in yi:
+                yi[q, h] = work.tile([128, H, 4], BF16, name="yi", bufs=4, align_bytes=64)
+            for b in blocks:
                 cols = slice(128 * b, 128 * b + 128)
                 nc.vector.tensor_scalar(
                     out=yi[q, h][:, cols, :].rearrange("p (c i) j -> p c j i", i=4),
@@ -177,33 +178,37 @@ def tile_lowrankplussoftthresholdedcrosscovarianc_d2p_kernel(
                         stop=(q == 1),
                     )
 
-        def diff(s, h):
-            for t in range(4):
-                col = slice(4 * s + t, 4 * s + t + 1)
-                e = deep.tile([128, H], F32, name="e_sb")
-                k = deep.tile([128, H], F32, name="k_sb")
-                k_sb[s, t, h] = k
-                nc.vector.scalar_tensor_tensor(
-                    out=e[:], in0=bank[s, t, h][:], scalar=gs[:, col], in1=f_sb[s, t, h][:], op0=ALU.mult, op1=ALU.subtract
-                )
-                nc.gpsimd.tensor_scalar(
-                    out=k[:], in0=e[:], scalar1=hi[:, col], scalar2=lo[:, col], op0=ALU.min, op1=ALU.max
-                )
+        def diff(s, h, t):
+            col = slice(4 * s + t, 4 * s + t + 1)
+            e = deep.tile([128, H], F32, name="e_sb")
+            k = deep.tile([128, H], F32, name="k_sb")
+            k_sb[s, t, h] = k
+            nc.vector.scalar_tensor_tensor(
+                out=e[:], in0=bank[s, t, h][:], scalar=gs[:, col], in1=f_sb[s, t, h][:], op0=ALU.mult, op1=ALU.subtract
+            )
+            nc.gpsimd.tensor_scalar(out=k[:], in0=e[:], scalar1=hi[:, col], scalar2=lo[:, col], op0=ALU.min, op1=ALU.max)
 
-        def shrink(s, h, lo_c, hi_c):
+        def shrink(s, h, t, lo_c=0, hi_c=H):
             if (s, h) not in sg:
                 sg[s, h] = work.tile([128, 4, H], BF16, name="sg", bufs=3, align_bytes=64)
-            if True:
-                cols = slice(lo_c, hi_c)
-                for t in range(4):
-                    nc.vector.scalar_tensor_tensor(
-                        out=sg[s, h][:, t, cols],
-                        in0=bank[s, t, h][:, cols],
-                        scalar=gs[:, 4 * s + t : 4 * s + t + 1],
-                        in1=k_sb[s, t, h][:, cols],
-                        op0=ALU.mult,
-                        op1=ALU.subtract,
-                    )
+            cols = slice(lo_c, hi_c)
+            nc.vector.scalar_tensor_tensor(
+                out=sg[s, h][:, t, cols],
+                in0=bank[s, t, h][:, cols],
+                scalar=gs[:, 4 * s + t : 4 * s + t + 1],
+                in1=k_sb[s, t, h][:, cols],
+                op0=ALU.mult,
+                op1=ALU.subtract,
+            )
+
+        def stream(h, lag, hooks):
+            for i in range(8 + lag):
+                if i < 8:
+                    diff(i // 4, h, i % 4)
+                if i >= lag:
+                    shrink((i - lag) // 4, h, (i - lag) % 4)
+                for hook in hooks.get(i, []):
+                    hook()
 
         def s_lay(s, h, lo_c, hi_c, engine_copy):
             if (s, h) not in si:
@@ -286,20 +291,19 @@ def tile_lowrankplussoftthresholdedcrosscovarianc_d2p_kernel(
                 )
 
         def row_factors():
-            nc.vector.tensor_copy(out=gf[:], in_=g_b[:])
-            nc.vector.tensor_tensor(out=gt[:], in0=g_b[:], in1=t_b[:], op=ALU.mult)
-            nc.vector.tensor_scalar(out=gs[:], in0=gf[:], scalar1=1.0 / T, scalar2=None, op0=ALU.mult)
-            nc.vector.tensor_scalar(out=ngt[:], in0=gt[:], scalar1=-1.0, scalar2=None, op0=ALU.mult)
-            nc.vector.tensor_tensor(out=hi[:], in0=gt[:], in1=ngt[:], op=ALU.max)
-            nc.vector.tensor_tensor(out=lo[:], in0=gt[:], in1=ngt[:], op=ALU.min)
+            nc.scalar.activation(out=gf[:], in_=g_b[:], func=COPY)
+            nc.scalar.activation(out=gs[:], in_=g_b[:], func=COPY, scale=1.0 / T)
+            nc.scalar.activation(out=ga[:], in_=g_b[:], func=mybir.ActivationFunctionType.Abs)
+            nc.gpsimd.tensor_tensor(out=hi[:], in0=ga[:], in1=t_b[:], op=ALU.mult)
+            nc.gpsimd.tensor_scalar(out=lo[:], in0=hi[:], scalar1=-1.0, scalar2=None, op0=ALU.mult)
 
         vcopy = nc.vector.tensor_copy
         scopy = nc.scalar.copy
 
-        x_lay(0, 0, vcopy, 2)
         row_factors()
+        x_lay(0, 0, vcopy, 2)
         y_widen(0, 0)
-        x_lay(1, 0)
+        x_lay(1, 0, vcopy, 2)
         y_widen(1, 0)
         x_quant(0, 0)
         x_quant(1, 0)
@@ -317,45 +321,25 @@ def tile_lowrankplussoftthresholdedcrosscovarianc_d2p_kernel(
         x_quant(1, 1)
         y_widen(0, 1)
         y_widen(1, 1)
-        diff(0, 0)
-        shrink(0, 0, 0, H)
         cross(1, 0)
-        y_lay_scalar(1, 1)
-        low_rank(0, 1)
-        y_lay(0, 1)
-        y_quant(0, 1)
+        stream(0, 3, {6: [lambda: y_lay_scalar(1, 1), lambda: y_lay_scalar(0, 1, range(4)), lambda: s_lay(0, 0, 0, H, scopy), lambda: low_rank(0, 1)]})
+        y_lay(0, 1, range(4, 4))
         y_quant(1, 1)
-        s_lay(0, 0, 0, H, scopy)
-        low_rank(1, 1)
-        diff(1, 0)
-        shrink(1, 0, 0, H)
+        y_quant(0, 1)
         cross(0, 1)
-        s_lay(1, 0, 0, H, scopy)
+        low_rank(1, 1)
         s_quant(0, 0, 0, H)
-        diff(0, 1)
-        shrink(0, 1, 0, H)
         cross(1, 1)
         exposure(0, 0)
-        s_lay(0, 1, 0, H, scopy)
+        stream(1, 3, {4: [lambda: s_lay(1, 0, 0, H, scopy)], 7: [lambda: s_lay(0, 1, 0, H, scopy)]})
         s_quant(1, 0, 0, H)
         exposure(1, 0)
-        store(0, False)
-        diff(1, 1)
-        s_quant(0, 1, 0, H)
-        shrink(1, 1, 0, 256)
-        shrink(1, 1, 256, 384)
         s_lay(1, 1, 0, 256, scopy)
-        s_lay(1, 1, 256, 384, scopy)
-        shrink(1, 1, 384, H)
+        s_quant(0, 1, 0, H)
+        exposure(0, 1)
+        s_lay(1, 1, 256, H, vcopy)
         s_quant(1, 1, 0, 256)
-        exposure_main(1, 0, 256)
-        s_lay(1, 1, 384, H, vcopy)
-        s_quant(1, 1, 256, 384)
-        exposure_main(1, 256, 384)
-        s_quant(1, 1, 384, H)
-        exposure_last(1)
-        store_main(1, 0, scopy)
-        store_main(1, 1, vcopy)
-        store_main(1, 2, scopy)
-        store_main(1, 3, vcopy)
-        store_last(1)
+        s_quant(1, 1, 256, H)
+        store(0, False)
+        exposure(1, 1)
+        store(1, True)

@@ -41,7 +41,6 @@ def tile_lowrankplussoftthresholdedcrosscovarianc_d2p_kernel(
         y_sc = {(q, h): keep.tile([128, H], U8, name=f"y_sc_{q}{h}", align_bytes=64) for q in range(2) for h in range(2)}
         s_code = {(s, h): keep.tile([128, H], U32, name=f"s_code_{s}{h}", align_bytes=64) for s in range(2) for h in range(2)}
         s_sc = {(s, h): keep.tile([128, H], U8, name=f"s_sc_{s}{h}", align_bytes=64) for s in range(2) for h in range(2)}
-        f_sb = {(s, t, h): keep.tile([128, H], F32, name=f"f_sb_{s}{t}{h}") for s in range(2) for t in range(4) for h in range(2)}
         l_sb = keep.tile([128, 2, 4, K], BF16, name="l_sb")
         m_sb = keep.tile([K, J], BF16, name="m_sb")
         lT = keep.tile([K, 8, 128], BF16, name="lT")
@@ -53,7 +52,7 @@ def tile_lowrankplussoftthresholdedcrosscovarianc_d2p_kernel(
         gs = keep.tile([128, 8], F32, name="gs")
         ga = keep.tile([128, 8], F32, name="ga")
         hi = keep.tile([128, 8], F32, name="hi")
-        lo = keep.tile([128, 8], F32, name="lo")
+        hi2 = keep.tile([128, 8], F32, name="hi2")
         ww = keep.tile([128, 2, 2 * P], U8, name="ww", align_bytes=64)
         wsc = keep.tile([128, 2, P], U8, name="wsc", align_bytes=64)
 
@@ -69,7 +68,7 @@ def tile_lowrankplussoftthresholdedcrosscovarianc_d2p_kernel(
 
         load_x(0, 0, 2)
         load_y(0, 0)
-        load_x(1, 0, 2)
+        load_x(1, 0)
         load_y(1, 0)
         nc.sync.dma_start(out=l_sb[:], in_=l.rearrange("(s p t) k -> p s t k", s=2, p=128, t=4))
         nc.sync.dma_start(out=m_sb[:], in_=m)
@@ -78,6 +77,12 @@ def tile_lowrankplussoftthresholdedcrosscovarianc_d2p_kernel(
         load_y(0, 1)
         load_y(1, 1)
         nc.sync.dma_start(out=ww[:].bitcast(I32), in_=w_words.bitcast(I32).rearrange("s p n -> p s n"))
+        nc.gpsimd.memset(wsc[:].bitcast(I32), 0)
+        for i in range(4):
+            nc.sync.dma_start(
+                out=wsc[32 * i : 32 * i + 4].bitcast(I32),
+                in_=w_scales[:, 4 * i : 4 * i + 4, :].bitcast(I32).rearrange("s r n -> r s n"),
+            )
 
         nc.scalar.dma_start(out=g_b[:].rearrange("p (s t) -> p s t", s=2), in_=g.rearrange("(s p t) -> p s t", s=2, p=128, t=4))
         nc.scalar.dma_start(out=t_b[:].rearrange("p (s t) -> p s t", s=2), in_=tau.rearrange("(s p t) -> p s t", s=2, p=128, t=4))
@@ -87,19 +92,14 @@ def tile_lowrankplussoftthresholdedcrosscovarianc_d2p_kernel(
             )
 
         make_identity(nc, ident[:])
-        nc.gpsimd.memset(wsc[:].bitcast(I32), 0)
-        for i in range(4):
-            nc.gpsimd.dma_start(
-                out=wsc[32 * i : 32 * i + 4].bitcast(I32),
-                in_=w_scales[:, 4 * i : 4 * i + 4, :].bitcast(I32).rearrange("s r n -> r s n"),
-            )
 
         xi = {}
         yw = {}
         yi = {}
         bank = {}
-        e_sb = {}
-        k_sb = {}
+        f_bank = {}
+        c_sb = {}
+        a_sb = {}
         sg = {}
         si = {}
 
@@ -161,7 +161,7 @@ def tile_lowrankplussoftthresholdedcrosscovarianc_d2p_kernel(
             for t in range(4):
                 ps = psum.tile([128, H], F32, name="ps_f", tag="ps")
                 nc.tensor.matmul(ps[:], lT[:, 4 * s + t, :], m_sb[:, h * H : (h + 1) * H], start=True, stop=True)
-                nc.scalar.activation(out=f_sb[s, t, h][:], in_=ps[:], func=COPY, scale=gf[:, 4 * s + t : 4 * s + t + 1])
+                f_bank[s, t, h] = ps
 
         def cross(s, h):
             for t in range(4):
@@ -178,37 +178,41 @@ def tile_lowrankplussoftthresholdedcrosscovarianc_d2p_kernel(
                         stop=(q == 1),
                     )
 
-        def diff(s, h, t):
-            col = slice(4 * s + t, 4 * s + t + 1)
-            e = deep.tile([128, H], F32, name="e_sb")
-            k = deep.tile([128, H], F32, name="k_sb")
-            k_sb[s, t, h] = k
-            nc.vector.scalar_tensor_tensor(
-                out=e[:], in0=bank[s, t, h][:], scalar=gs[:, col], in1=f_sb[s, t, h][:], op0=ALU.mult, op1=ALU.subtract
-            )
-            nc.gpsimd.tensor_scalar(out=k[:], in0=e[:], scalar1=hi[:, col], scalar2=lo[:, col], op0=ALU.min, op1=ALU.max)
+        def evac(s, h):
+            for t in range(4):
+                col = slice(4 * s + t, 4 * s + t + 1)
+                c_up = deep.tile([128, H], F32, name="c_up")
+                c_sb[s, t, h] = c_up
+                nc.scalar.activation(
+                    out=c_up[:], in_=bank[s, t, h][:], func=mybir.ActivationFunctionType.Identity, scale=gs[:, col], bias=hi[:, col]
+                )
 
-        def shrink(s, h, t, lo_c=0, hi_c=H):
+        def cap(s, h, t):
+            a = deep.tile([128, H], F32, name="a_sb", bufs=4)
+            a_sb[s, t, h] = a
+            nc.vector.scalar_tensor_tensor(
+                out=a[:], in0=f_bank[s, t, h][:], scalar=gf[:, 4 * s + t : 4 * s + t + 1], in1=c_sb[s, t, h][:], op0=ALU.mult, op1=ALU.min
+            )
+
+        def floor(s, h, t, lo_c=0, hi_c=H):
             if (s, h) not in sg:
                 sg[s, h] = work.tile([128, 4, H], BF16, name="sg", bufs=3, align_bytes=64)
             cols = slice(lo_c, hi_c)
             nc.vector.scalar_tensor_tensor(
                 out=sg[s, h][:, t, cols],
-                in0=bank[s, t, h][:, cols],
-                scalar=gs[:, 4 * s + t : 4 * s + t + 1],
-                in1=k_sb[s, t, h][:, cols],
-                op0=ALU.mult,
-                op1=ALU.subtract,
+                in0=c_sb[s, t, h][:, cols],
+                scalar=hi2[:, 4 * s + t : 4 * s + t + 1],
+                in1=a_sb[s, t, h][:, cols],
+                op0=ALU.subtract,
+                op1=ALU.max,
             )
 
-        def stream(h, lag, hooks):
-            for i in range(8 + lag):
-                if i < 8:
-                    diff(i // 4, h, i % 4)
-                if i >= lag:
-                    shrink((i - lag) // 4, h, (i - lag) % 4)
-                for hook in hooks.get(i, []):
-                    hook()
+        def clip(s, h, lag=1):
+            for t in range(4 + lag):
+                if t < 4:
+                    cap(s, h, t)
+                if t >= lag:
+                    floor(s, h, t - lag)
 
         def s_lay(s, h, lo_c, hi_c, engine_copy):
             if (s, h) not in si:
@@ -294,8 +298,15 @@ def tile_lowrankplussoftthresholdedcrosscovarianc_d2p_kernel(
             nc.scalar.activation(out=gf[:], in_=g_b[:], func=COPY)
             nc.scalar.activation(out=gs[:], in_=g_b[:], func=COPY, scale=1.0 / T)
             nc.scalar.activation(out=ga[:], in_=g_b[:], func=mybir.ActivationFunctionType.Abs)
-            nc.gpsimd.tensor_tensor(out=hi[:], in0=ga[:], in1=t_b[:], op=ALU.mult)
-            nc.gpsimd.tensor_scalar(out=lo[:], in0=hi[:], scalar1=-1.0, scalar2=None, op0=ALU.mult)
+
+        def thresholds():
+            nc.vector.tensor_tensor(out=hi[:], in0=ga[:], in1=t_b[:], op=ALU.mult)
+            nc.vector.tensor_scalar(out=hi2[:], in0=hi[:], scalar1=2.0, scalar2=None, op0=ALU.mult)
+
+        def warm(s, h, t, lo_c, hi_c):
+            if t == 0 and lo_c == 0:
+                bank["warm"] = psum.tile([128, H], F32, name="ps_w", tag="ps")
+            nc.tensor.matmul(bank["warm"][:, lo_c:hi_c], ident[:], sg[s, h][:, t, lo_c:hi_c], start=True, stop=True)
 
         vcopy = nc.vector.tensor_copy
         scopy = nc.scalar.copy
@@ -303,43 +314,61 @@ def tile_lowrankplussoftthresholdedcrosscovarianc_d2p_kernel(
         row_factors()
         x_lay(0, 0, vcopy, 2)
         y_widen(0, 0)
-        x_lay(1, 0, vcopy, 2)
+        thresholds()
+        x_lay(1, 0)
         y_widen(1, 0)
         x_quant(0, 0)
         x_quant(1, 0)
         low_rank_weights()
         y_lay(0, 0)
         y_lay(1, 0)
-        low_rank(0, 0)
-        low_rank(1, 0)
+        y_widen(0, 1)
         y_quant(0, 0)
         y_quant(1, 0)
         cross(0, 0)
+        low_rank(0, 0)
         x_lay(0, 1)
         x_lay(1, 1)
+        evac(0, 0)
         x_quant(0, 1)
         x_quant(1, 1)
-        y_widen(0, 1)
         y_widen(1, 1)
         cross(1, 0)
-        stream(0, 3, {6: [lambda: y_lay_scalar(1, 1), lambda: y_lay_scalar(0, 1, range(4)), lambda: s_lay(0, 0, 0, H, scopy), lambda: low_rank(0, 1)]})
-        y_lay(0, 1, range(4, 4))
+        clip(0, 0)
+        low_rank(1, 0)
+        y_lay_scalar(1, 1)
+        y_lay_scalar(0, 1, range(2))
+        y_lay(0, 1, range(2, 4))
         y_quant(1, 1)
         y_quant(0, 1)
+        evac(1, 0)
         cross(0, 1)
-        low_rank(1, 1)
-        s_quant(0, 0, 0, H)
+        s_lay(0, 0, 0, H, scopy)
+        clip(1, 0)
+        evac(0, 1)
+        low_rank(0, 1)
         cross(1, 1)
+        s_quant(0, 0, 0, H)
         exposure(0, 0)
-        stream(1, 3, {4: [lambda: s_lay(1, 0, 0, H, scopy)], 7: [lambda: s_lay(0, 1, 0, H, scopy)]})
+        clip(0, 1)
+        s_lay(1, 0, 0, H, scopy)
+        evac(1, 1)
+        low_rank(1, 1)
         s_quant(1, 0, 0, H)
         exposure(1, 0)
+        s_lay(0, 1, 0, H, scopy)
+        cap(1, 1, 0)
+        cap(1, 1, 1)
+        cap(1, 1, 2)
+        cap(1, 1, 3)
+        for t in range(4): floor(1, 1, t, 0, 256); warm(1, 1, t, 0, 256)
+        for t in range(4): floor(1, 1, t, 256, H); warm(1, 1, t, 256, H)
+        store(0, False)
         s_lay(1, 1, 0, 256, scopy)
         s_quant(0, 1, 0, H)
         exposure(0, 1)
         s_lay(1, 1, 256, H, vcopy)
         s_quant(1, 1, 0, 256)
         s_quant(1, 1, 256, H)
-        store(0, False)
         exposure(1, 1)
         store(1, True)

@@ -68,10 +68,12 @@ def tile_lowrankplussoftthresholdedcrosscovarianc_d2p_kernel(
 
         load_x(0, 0, 2)
         load_y(0, 0)
-        load_x(1, 0)
+        load_x(1, 0, 2)
         load_y(1, 0)
         nc.sync.dma_start(out=l_sb[:], in_=l.rearrange("(s p t) k -> p s t k", s=2, p=128, t=4))
         nc.sync.dma_start(out=m_sb[:], in_=m)
+        nc.sync.dma_start(out=g_b[:].rearrange("p (s t) -> p s t", s=2), in_=g.rearrange("(s p t) -> p s t", s=2, p=128, t=4))
+        nc.sync.dma_start(out=t_b[:].rearrange("p (s t) -> p s t", s=2), in_=tau.rearrange("(s p t) -> p s t", s=2, p=128, t=4))
         load_x(0, 1)
         load_x(1, 1)
         load_y(0, 1)
@@ -84,8 +86,6 @@ def tile_lowrankplussoftthresholdedcrosscovarianc_d2p_kernel(
                 in_=w_scales[:, 4 * i : 4 * i + 4, :].bitcast(I32).rearrange("s r n -> r s n"),
             )
 
-        nc.scalar.dma_start(out=g_b[:].rearrange("p (s t) -> p s t", s=2), in_=g.rearrange("(s p t) -> p s t", s=2, p=128, t=4))
-        nc.scalar.dma_start(out=t_b[:].rearrange("p (s t) -> p s t", s=2), in_=tau.rearrange("(s p t) -> p s t", s=2, p=128, t=4))
         for i in range(4):
             nc.scalar.dma_start(
                 out=ysc[32 * i : 32 * i + 32], in_=y_scale.rearrange("(q i) b -> i q b", i=4)[i].partition_broadcast(32)
@@ -301,7 +301,7 @@ def tile_lowrankplussoftthresholdedcrosscovarianc_d2p_kernel(
 
         def thresholds():
             nc.vector.tensor_tensor(out=hi[:], in0=ga[:], in1=t_b[:], op=ALU.mult)
-            nc.vector.tensor_scalar(out=hi2[:], in0=hi[:], scalar1=2.0, scalar2=None, op0=ALU.mult)
+            nc.vector.scalar_tensor_tensor(out=hi2[:], in0=t_b[:], scalar=2.0, in1=ga[:], op0=ALU.mult, op1=ALU.mult)
 
         def warm(s, h, t, lo_c, hi_c):
             if t == 0 and lo_c == 0:
@@ -311,18 +311,18 @@ def tile_lowrankplussoftthresholdedcrosscovarianc_d2p_kernel(
         vcopy = nc.vector.tensor_copy
         scopy = nc.scalar.copy
 
-        row_factors()
         x_lay(0, 0, vcopy, 2)
         y_widen(0, 0)
-        thresholds()
-        x_lay(1, 0)
+        x_lay(1, 0, vcopy, 2)
         y_widen(1, 0)
         x_quant(0, 0)
         x_quant(1, 0)
         low_rank_weights()
+        row_factors()
         y_lay(0, 0)
         y_lay(1, 0)
         y_widen(0, 1)
+        thresholds()
         y_quant(0, 0)
         y_quant(1, 0)
         cross(0, 0)
@@ -365,9 +365,10 @@ def tile_lowrankplussoftthresholdedcrosscovarianc_d2p_kernel(
         for t in range(4): floor(1, 1, t, 256, H); warm(1, 1, t, 256, H)
         store(0, False)
         s_lay(1, 1, 0, 256, scopy)
+        s_lay(1, 1, 256, 384, scopy)
         s_quant(0, 1, 0, H)
         exposure(0, 1)
-        s_lay(1, 1, 256, H, vcopy)
+        s_lay(1, 1, 384, H, vcopy)
         s_quant(1, 1, 0, 256)
         s_quant(1, 1, 256, H)
         exposure(1, 1)

from contextlib import ExitStack

import concourse.mybir as mybir
from concourse.masks import make_identity

F32 = mybir.dt.float32
BF16 = mybir.dt.bfloat16
U8 = mybir.dt.uint8
U32 = mybir.dt.uint32
I32 = mybir.dt.int32
FP8 = mybir.dt.float8_e4m3fn
FP8X4 = mybir.dt.float8_e4m3fn_x4
FP4X4 = mybir.dt.float4_e2m1fn_x4
ALU = mybir.AluOpType
COPY = mybir.ActivationFunctionType.Copy

T, N, J, K, P = 1024, 1024, 1024, 128, 512
FLOPS = 2 * T * N * J + 2 * N * K * J + 2 * P * N * J
H = 512


def tile_lowrankplussoftthresholdedcrosscovarianc_d2p_kernel(
    tc, x, y_bytes, y_scale, l, m, tau, g, w_words, w_scales, out
):
    nc = tc.nc
    with ExitStack() as ctx:
        keep = ctx.enter_context(tc.tile_pool(name="keep", bufs=1))
        work = ctx.enter_context(tc.tile_pool(name="work", bufs=2))
        deep = ctx.enter_context(tc.tile_pool(name="deep", bufs=8))
        psum = ctx.enter_context(tc.psum_pool(name="psum", bufs=8))
        ctx.enter_context(tc.manual_schedule())

        x_v = x.rearrange("(q p j) n -> q p j n", q=2, p=128, j=4)
        y_v = y_bytes.rearrange("(q p j) n -> q p j n", q=2, p=128, j=4)

        x_raw = {(q, s): keep.tile([128, 4, H], BF16, name=f"x_raw_{q}{s}", align_bytes=64) for q in range(2) for s in range(2)}
        y_raw = {(q, h): keep.tile([128, 4, H], U8, name=f"y_raw_{q}{h}", align_bytes=64) for q in range(2) for h in range(2)}
        x_code = {(q, s): keep.tile([128, H], U32, name=f"x_code_{q}{s}", align_bytes=64) for q in range(2) for s in range(2)}
        x_sc = {(q, s): keep.tile([128, H], U8, name=f"x_sc_{q}{s}", align_bytes=64) for q in range(2) for s in range(2)}
        y_code = {(q, h): keep.tile([128, H], U32, name=f"y_code_{q}{h}", align_bytes=64) for q in range(2) for h in range(2)}
        y_sc = {(q, h): keep.tile([128, H], U8, name=f"y_sc_{q}{h}", align_bytes=64) for q in range(2) for h in range(2)}
        s_code = {(s, h): keep.tile([128, H], U32, name=f"s_code_{s}{h}", align_bytes=64) for s in range(2) for h in range(2)}
        s_sc = {(s, h): keep.tile([128, H], U8, name=f"s_sc_{s}{h}", align_bytes=64) for s in range(2) for h in range(2)}
        l_sb = keep.tile([128, 2, 4, K], BF16, name="l_sb")
        m_sb = keep.tile([K, J], BF16, name="m_sb")
        lT = keep.tile([K, 8, 128], BF16, name="lT")
        ident = keep.tile([128, 128], BF16, name="ident")
        ysc = keep.tile([128, 2, 8], F32, name="ysc")
        g_b = keep.tile([128, 8], BF16, name="g_b")
        t_b = keep.tile([128, 8], BF16, name="t_b")
        gf = keep.tile([128, 8], F32, name="gf")
        gs = keep.tile([128, 8], F32, name="gs")
        ga = keep.tile([128, 8], F32, name="ga")
        hi = keep.tile([128, 8], F32, name="hi")
        hi2 = keep.tile([128, 8], F32, name="hi2")
        ww = keep.tile([128, 2, 2 * P], U8, name="ww", align_bytes=64)
        wsc = keep.tile([128, 2, P], U8, name="wsc", align_bytes=64)

        def load_x(q, s, parts=1):
            w = H // parts
            for c in range(parts):
                nc.sync.dma_start(
                    out=x_raw[q, s][:, :, c * w : (c + 1) * w], in_=x_v[q][:, :, s * H + c * w : s * H + (c + 1) * w]
                )

        def load_y(q, h):
            nc.sync.dma_start(out=y_raw[q, h][:], in_=y_v[q][:, :, h * H : (h + 1) * H])

        load_x(0, 0, 2)
        load_y(0, 0)
        load_x(1, 0, 2)
        load_y(1, 0)
        nc.sync.dma_start(out=l_sb[:], in_=l.rearrange("(s p t) k -> p s t k", s=2, p=128, t=4))
        nc.sync.dma_start(out=m_sb[:], in_=m)
        nc.sync.dma_start(out=g_b[:].rearrange("p (s t) -> p s t", s=2), in_=g.rearrange("(s p t) -> p s t", s=2, p=128, t=4))
        nc.sync.dma_start(out=t_b[:].rearrange("p (s t) -> p s t", s=2), in_=tau.rearrange("(s p t) -> p s t", s=2, p=128, t=4))
        load_x(0, 1)
        load_x(1, 1)
        load_y(0, 1)
        load_y(1, 1)
        nc.sync.dma_start(out=ww[:].bitcast(I32), in_=w_words.bitcast(I32).rearrange("s p n -> p s n"))
        nc.gpsimd.memset(wsc[:].bitcast(I32), 0)
        for i in range(4):
            nc.sync.dma_start(
                out=wsc[32 * i : 32 * i + 4].bitcast(I32),
                in_=w_scales[:, 4 * i : 4 * i + 4, :].bitcast(I32).rearrange("s r n -> r s n"),
            )

        for i in range(4):
            nc.scalar.dma_start(
                out=ysc[32 * i : 32 * i + 32], in_=y_scale.rearrange("(q i) b -> i q b", i=4)[i].partition_broadcast(32)
            )

        make_identity(nc, ident[:])

        xi = {}
        yw = {}
        yi = {}
        bank = {}
        f_bank = {}
        c_sb = {}
        a_sb = {}
        sg = {}
        si = {}

        def x_lay(q, s, engine_copy=nc.vector.tensor_copy, parts=1):
            xi[q, s] = work.tile([128, 4 * H], BF16, name="xi", bufs=4, align_bytes=64)
            dst = xi[q, s][:].rearrange("p (t m j) -> p t m j", t=4, j=4)
            src = x_raw[q, s][:].rearrange("p j (m t) -> p t m j", t=4)
            w = 128 // parts
            for c in range(parts):
                engine_copy(out=dst[:, :, c * w : (c + 1) * w, :], in_=src[:, :, c * w : (c + 1) * w, :])

        def x_quant(q, s):
            nc.vector.quantize_mx(out=x_code[q, s][:].bitcast(FP8X4), scales=x_sc[q, s][:], in_=xi[q, s][:])

        def y_widen(q, h):
            yw[q, h] = work.tile([128, 4, H], BF16, name="yw", bufs=4, align_bytes=64)
            nc.scalar.copy(
                out=yw[q, h][:].rearrange("p j n -> p (j n)"), in_=y_raw[q, h][:].rearrange("p j n -> p (j n)").bitcast(FP8)
            )

        def y_lay_scalar(q, h, blocks=range(4)):
            if (q, h) not in yi:
                yi[q, h] = work.tile([128, H, 4], BF16, name="yi", bufs=4, align_bytes=64)
            for b in blocks:
                cols = slice(128 * b, 128 * b + 128)
                nc.scalar.activation(
                    out=yi[q, h][:, cols, :].rearrange("p (c i) j -> p c j i", i=4),
                    in_=yw[q, h][:, :, cols].rearrange("p j (c i) -> p c j i", i=4),
                    func=COPY,
                    scale=ysc[:, q, 4 * h + b : 4 * h + b + 1],
                )

        def y_lay(q, h, blocks=range(4)):
            if (q, h) not in yi:
                yi[q, h] = work.tile([128, H, 4], BF16, name="yi", bufs=4, align_bytes=64)
            for b in blocks:
                cols = slice(128 * b, 128 * b + 128)
                nc.vector.tensor_scalar(
                    out=yi[q, h][:, cols, :].rearrange("p (c i) j -> p c j i", i=4),
                    in0=yw[q, h][:, :, cols].rearrange("p j (c i) -> p c j i", i=4),
                    scalar1=ysc[:, q, 4 * h + b : 4 * h + b + 1],
                    scalar2=None,
                    op0=ALU.mult,
                )

        def y_quant(q, h):
            nc.vector.quantize_mx(
                out=y_code[q, h][:].bitcast(FP8X4), scales=y_sc[q, h][:], in_=yi[q, h][:].rearrange("p n j -> p (n j)")
            )

        def low_rank_weights():
            for s in range(2):
                ps = psum.tile([128, 512], BF16, name="ps_l", tag="ps")
                for t in range(4):
                    nc.tensor.transpose(ps[:, 128 * t : 128 * t + 128], l_sb[:, s, t, :], ident[:])
                nc.scalar.copy(out=lT[:, 4 * s : 4 * s + 4, :].rearrange("p t n -> p (t n)"), in_=ps[:])

        def low_rank(s, h):
            for t in range(4):
                ps = psum.tile([128, H], F32, name="ps_f", tag="ps")
                nc.tensor.matmul(ps[:], lT[:, 4 * s + t, :], m_sb[:, h * H : (h + 1) * H], start=True, stop=True)
                f_bank[s, t, h] = ps

        def cross(s, h):
            for t in range(4):
                ps = psum.tile([128, H], F32, name="ps_c", tag="ps")
                bank[s, t, h] = ps
                for q in range(2):
                    nc.tensor.matmul_mx(
                        out=ps[:],
                        lhsT=x_code[q, s][:, 128 * t : 128 * t + 128].bitcast(FP8X4),
                        lhsT_scale=x_sc[q, s][:, 128 * t : 128 * t + 128],
                        rhs=y_code[q, h][:].bitcast(FP8X4),
                        rhs_scale=y_sc[q, h][:],
                        start=(q == 0),
                        stop=(q == 1),
                    )

        def evac(s, h):
            for t in range(4):
                col = slice(4 * s + t, 4 * s + t + 1)
                c_up = deep.tile([128, H], F32, name="c_up")
                c_sb[s, t, h] = c_up
                nc.scalar.activation(
                    out=c_up[:], in_=bank[s, t, h][:], func=mybir.ActivationFunctionType.Identity, scale=gs[:, col], bias=hi[:, col]
                )

        def cap(s, h, t):
            a = deep.tile([128, H], F32, name="a_sb", bufs=4)
            a_sb[s, t, h] = a
            nc.vector.scalar_tensor_tensor(
                out=a[:], in0=f_bank[s, t, h][:], scalar=gf[:, 4 * s + t : 4 * s + t + 1], in1=c_sb[s, t, h][:], op0=ALU.mult, op1=ALU.min
            )

        def floor(s, h, t, lo_c=0, hi_c=H):
            if (s, h) not in sg:
                sg[s, h] = work.tile([128, 4, H], BF16, name="sg", bufs=3, align_bytes=64)
            cols = slice(lo_c, hi_c)
            nc.vector.scalar_tensor_tensor(
                out=sg[s, h][:, t, cols],
                in0=c_sb[s, t, h][:, cols],
                scalar=hi2[:, 4 * s + t : 4 * s + t + 1],
                in1=a_sb[s, t, h][:, cols],
                op0=ALU.subtract,
                op1=ALU.max,
            )

        def clip(s, h, lag=1):
            for t in range(4 + lag):
                if t < 4:
                    cap(s, h, t)
                if t >= lag:
                    floor(s, h, t - lag)

        def s_lay(s, h, lo_c, hi_c, engine_copy):
            if (s, h) not in si:
                si[s, h] = work.tile([128, H, 4], BF16, name="si", bufs=3, align_bytes=64)
            engine_copy(
                out=si[s, h][:, lo_c:hi_c, :].rearrange("p (c i) t -> p c t i", i=4),
                in_=sg[s, h][:, :, lo_c:hi_c].rearrange("p t (c i) -> p c t i", i=4),
            )

        def s_quant(s, h, lo_c, hi_c):
            nc.vector.quantize_mx(
                out=s_code[s, h][:, lo_c:hi_c].bitcast(FP8X4),
                scales=s_sc[s, h][:, lo_c:hi_c],
                in_=si[s, h][:, lo_c:hi_c, :].rearrange("p n t -> p (n t)"),
            )

        acc = {}

        def exposure(s, h):
            for b in range(4):
                if s == 0:
                    acc[b, h] = psum.tile([128, H], F32, name="ps_o", tag="ps")
                nc.tensor.matmul_mx(
                    out=acc[b, h][:],
                    lhsT=ww[:, s, 256 * b : 256 * b + 256].bitcast(FP4X4),
                    lhsT_scale=wsc[:, s, 128 * b : 128 * b + 128],
                    rhs=s_code[s, h][:].bitcast(FP8X4),
                    rhs_scale=s_sc[s, h][:],
                    start=(s == 0),
                    stop=(s == 1),
                )

        def store(h, vector_too):
            for b in range(4):
                o = deep.tile([128, H], F32, name="o_sb")
                if vector_too and b % 2 == 1:
                    nc.vector.tensor_copy(out=o[:], in_=acc[b, h][:])
                else:
                    nc.scalar.copy(out=o[:], in_=acc[b, h][:])
                nc.sync.dma_start(out=out[128 * b : 128 * b + 128, h * H : (h + 1) * H], in_=o[:])

        def exposure_cols(bank_of, h, lo_c, hi_c):
            for c in range(lo_c, hi_c, 128):
                for b in range(4):
                    for s in range(2):
                        nc.tensor.matmul_mx(
                            out=bank_of(b, c),
                            lhsT=ww[:, s, 256 * b : 256 * b + 256].bitcast(FP4X4),
                            lhsT_scale=wsc[:, s, 128 * b : 128 * b + 128],
                            rhs=s_code[s, h][:, c : c + 128].bitcast(FP8X4),
                            rhs_scale=s_sc[s, h][:, c : c + 128],
                            start=(s == 0),
                            stop=(s == 1),
                        )

        tail = {}

        def exposure_main(h, lo_c, hi_c):
            if lo_c == 0:
                for b in range(4):
                    tail[b] = psum.tile([128, H], F32, name="ps_m", tag="ps")
            exposure_cols(lambda b, c: tail[b][:, c : c + 128], h, lo_c, hi_c)

        def exposure_last(h):
            for b in range(2):
                tail[4 + b] = psum.tile([128, H], F32, name="ps_t", tag="ps")
            exposure_cols(lambda b, c: tail[4 + b // 2][:, 128 * (b % 2) : 128 * (b % 2) + 128], h, H - 128, H)

        def store_main(h, b, engine_copy):
            o = deep.tile([128, H - 128], F32, name="o_main", bufs=4)
            engine_copy(out=o[:], in_=tail[b][:, : H - 128])
            nc.sync.dma_start(out=out[128 * b : 128 * b + 128, h * H : h * H + H - 128], in_=o[:])

        def store_last(h):
            for b, engine_copy in ((0, vcopy), (1, scopy)):
                o = deep.tile([128, 2, 128], F32, name="o_last", bufs=2)
                engine_copy(out=o[:].rearrange("p b n -> p (b n)"), in_=tail[4 + b][:, :256])
                nc.sync.dma_start(
                    out=out[256 * b : 256 * b + 256, h * H + H - 128 : h * H + H].rearrange("(b p) n -> p b n", b=2), in_=o[:]
                )

        def row_factors():
            nc.scalar.activation(out=gf[:], in_=g_b[:], func=COPY)
            nc.scalar.activation(out=gs[:], in_=g_b[:], func=COPY, scale=1.0 / T)
            nc.scalar.activation(out=ga[:], in_=g_b[:], func=mybir.ActivationFunctionType.Abs)

        def thresholds():
            nc.vector.tensor_tensor(out=hi[:], in0=ga[:], in1=t_b[:], op=ALU.mult)
            nc.vector.scalar_tensor_tensor(out=hi2[:], in0=t_b[:], scalar=2.0, in1=ga[:], op0=ALU.mult, op1=ALU.mult)

        def warm(s, h, t, lo_c, hi_c):
            if t == 0 and lo_c == 0:
                bank["warm"] = psum.tile([128, H], F32, name="ps_w", tag="ps")
            nc.tensor.matmul(bank["warm"][:, lo_c:hi_c], ident[:], sg[s, h][:, t, lo_c:hi_c], start=True, stop=True)

        vcopy = nc.vector.tensor_copy
        scopy = nc.scalar.copy

        x_lay(0, 0, vcopy, 2)
        y_widen(0, 0)
        x_lay(1, 0, vcopy, 2)
        y_widen(1, 0)
        x_quant(0, 0)
        x_quant(1, 0)
        low_rank_weights()
        row_factors()
        y_lay(0, 0)
        y_lay(1, 0)
        y_widen(0, 1)
        thresholds()
        y_quant(0, 0)
        y_quant(1, 0)
        cross(0, 0)
        low_rank(0, 0)
        x_lay(0, 1)
        x_lay(1, 1)
        evac(0, 0)
        x_quant(0, 1)
        x_quant(1, 1)
        y_widen(1, 1)
        cross(1, 0)
        clip(0, 0)
        low_rank(1, 0)
        y_lay_scalar(1, 1)
        y_lay_scalar(0, 1, range(2))
        y_lay(0, 1, range(2, 4))
        y_quant(1, 1)
        y_quant(0, 1)
        evac(1, 0)
        cross(0, 1)
        s_lay(0, 0, 0, H, scopy)
        clip(1, 0)
        evac(0, 1)
        low_rank(0, 1)
        cross(1, 1)
        s_quant(0, 0, 0, H)
        exposure(0, 0)
        clip(0, 1)
        s_lay(1, 0, 0, H, scopy)
        evac(1, 1)
        low_rank(1, 1)
        s_quant(1, 0, 0, H)
        exposure(1, 0)
        s_lay(0, 1, 0, H, scopy)
        cap(1, 1, 0)
        cap(1, 1, 1)
        cap(1, 1, 2)
        cap(1, 1, 3)
        for t in range(4): floor(1, 1, t, 0, 256); warm(1, 1, t, 0, 256)
        for t in range(4): floor(1, 1, t, 256, H); warm(1, 1, t, 256, H)
        store(0, False)
        s_lay(1, 1, 0, 256, scopy)
        s_lay(1, 1, 256, 384, scopy)
        s_quant(0, 1, 0, H)
        exposure(0, 1)
        s_lay(1, 1, 384, H, vcopy)
        s_quant(1, 1, 0, 256)
        s_quant(1, 1, 256, H)
        exposure(1, 1)
        store(1, True)
